import numpy as np
import ml_dtypes


def mxq(x, axis, fmt="e4m3"):
    dtype, down = {"e4m3": (ml_dtypes.float8_e4m3fn, 7), "e5m2": (ml_dtypes.float8_e5m2, 14)}[fmt]
    v = np.moveaxis(np.asarray(x, np.float32).astype(ml_dtypes.bfloat16).astype(np.float64), axis, -1)
    blocks = v.reshape(v.shape[:-1] + (-1, 32))
    amax = np.abs(blocks).max(-1, keepdims=True)
    byte = np.maximum(np.where(amax > 0, np.frexp(amax)[1] - 1 + 127, 0) - down, 1)
    scale = np.exp2(byte - 127.0)
    codes = (blocks / scale).astype(np.float32).astype(dtype).astype(np.float64)
    return np.moveaxis((codes * scale).reshape(v.shape), -1, axis)


WIDE = False


def mx_kscale(k):
    if not WIDE:
        return np.ones(k)
    levels = np.array([10, -10, 5, -5, 0])
    if k % 512:
        return np.exp2(np.random.permutation(np.resize(levels, k // 32))).repeat(32)
    a = np.empty((k // 512, 16))
    for p in range(k // 512):
        a[p, :8] = np.random.permutation(np.resize(levels, 8))
        for g in range(8):
            far = levels[np.abs(levels - a[p, g]) >= 10]
            a[p, g + 8] = far[np.random.randint(len(far))]
    return np.exp2(a.ravel()).repeat(32)


def f64(x):
    return np.asarray(x).astype(np.float64)


def striped(idx):
    return np.tile(idx.reshape(-1, 16).T, (8, 1)).astype(np.uint16)


def unstriped(offs):
    return offs[:16].T.reshape(-1).astype(np.int64)


def striped8(idx):
    return np.concatenate([x.reshape(-1, 16).T for x in idx]).astype(np.uint16)


def runs(offs, k):
    lists = np.stack([offs[16 * r : 16 * r + 16].T.reshape(-1) for r in range(8)]).astype(np.int64)
    return lists[np.arange(k) % 512 // 64]


def pack_weight(w):
    k, n = w.shape
    w = f64(np.asarray(w, np.float32).astype(ml_dtypes.bfloat16)).reshape(k // 32, 32, n)
    amax = np.abs(w).max(1)
    byte = np.clip(np.where(amax > 0, np.frexp(amax)[1] - 1 + 127 - 7, 1), 1, 254)
    scaled = (w * np.exp2(127.0 - byte)[:, None, :]).reshape(k, n).astype(np.float32)
    words = np.ascontiguousarray(scaled.reshape(k // 512, 128, 4, n).transpose(0, 1, 3, 2)).astype(ml_dtypes.float8_e4m3fn).view(np.uint8)
    return words, np.ascontiguousarray(byte.astype(np.uint8).reshape(k // 512, 16, n))


def unpack_weight(words, scales):
    g, p, n, _ = words.shape
    vals = np.ascontiguousarray(words).view(ml_dtypes.float8_e4m3fn).astype(np.float64) * np.repeat(np.exp2(scales.astype(np.float64) - 127.0), 8, axis=1)[..., None]
    return vals.transpose(0, 1, 3, 2).reshape(g * 512, n)


K, T, S, H, G = 512, 2048, 512, 512, 2048


def setup_inputs():
    n = np.random.standard_normal
    s = mx_kscale(K)[:, None]
    packed_xT = pack_weight(n((K, T)) * s)
    packed_dT = pack_weight(n((K, G)) / s)
    return {
        "x_words": packed_xT[0],
        "x_scales": packed_xT[1],
        "w1": (n((K, H)) / np.sqrt(K) / s).astype(np.float32),
        "w2": (n((K, H)) / np.sqrt(K) / s).astype(np.float32),
        "gs": (np.random.uniform(0.5, 1.5, (K, 1)) * s).astype(np.float32),
        "d_words": packed_dT[0],
        "d_scales": packed_dT[1],
        "offs": striped(np.random.permutation(T)[:S]),
        "two": striped(np.random.permutation(T)[:S]),
        "nb": striped8(np.stack([np.random.permutation(S) for _ in range(8)])),
        "kq": striped8(np.random.randint(0, G, (8, H))),
    }


def reference(x_words, x_scales, w1, w2, gs, d_words, d_scales, offs, two, nb, kq):
    d_kq = unpack_weight(d_words, d_scales)[np.arange(K)[:, None], runs(kq, K)]
    x_two = unpack_weight(x_words, x_scales)[:, unstriped(two)]
    c = mxq(f64(w2), 0, "e4m3").T @ x_two
    xq = unpack_weight(x_words, x_scales)[:, unstriped(offs)]
    y = mxq(f64(w1), 0, "e4m3").T @ xq
    vn = c - (np.tanh(y - (y[np.arange(H)[:, None], runs(nb, H)])))
    xn = y + 0.5 * vn
    z = f64(gs) * (vn - (np.tanh(xn - (xn[np.arange(H)[:, None], runs(nb, H)]))))
    return 0.0625 * ((d_kq.T @ mxq(z, 0, "e4m3")))

@@ -1,0 +1,195 @@
+from contextlib import ExitStack
+
+import concourse.mybir as mybir
+
+K, T, S, H, G = 512, 2048, 512, 512, 2048
+FLOPS = 3 * 2 * K * H * S
+
+F32 = mybir.dt.float32
+BF16 = mybir.dt.bfloat16
+I32 = mybir.dt.int32
+U32 = mybir.dt.uint32
+U16 = mybir.dt.uint16
+U8 = mybir.dt.uint8
+FP8X4 = mybir.dt.float8_e4m3fn_x4
+ACT = mybir.ActivationFunctionType
+ALU = mybir.AluOpType
+
+P = 128
+PACK = 4
+HALF = S // 2
+
+
+def tile_picked_symplec_none_p_kernel(
+    tc, x_words, x_scales, w1, w2, gs, d_words, d_scales, offs, two, nb, kq, out
+):
+    nc = tc.nc
+    with ExitStack() as ctx:
+        sb = ctx.enter_context(tc.tile_pool(name="sb", bufs=1))
+        ps = ctx.enter_context(tc.psum_pool(name="ps", bufs=1))
+
+        def tile(name, shape, dtype):
+            return sb.tile(shape, dtype, name=name, align_bytes=64)
+
+        def load_list(name, src):
+            dst = tile(name, [P, S // 16], U16)
+            nc.sync.dma_start(dst[:], src)
+            return dst
+
+        def load_words(name, src):
+            dst = tile(name, [P, T], I32)
+            nc.sync.dma_start(dst[:], src[0].rearrange("p n r -> p (n r)").bitcast(I32))
+            return dst
+
+        def load_weight_half(name, src, h):
+            dst = tile(name, [P, PACK, HALF], F32)
+            nc.sync.dma_start(dst[:], src.rearrange("(p j) c -> p j c", j=PACK)[:, :, h * HALF : (h + 1) * HALF])
+            return dst
+
+        zero = tile("zero", [P, 1], F32)
+        nc.vector.memset(zero[:], 0.0)
+        bias0 = tile("bias0", [P, 1], F32)
+        nc.scalar.activation(bias0[:], zero[:], ACT.Tanh)
+
+        xs_tab = tile("xs_tab", [P, T], U8)
+        ds_tab = tile("ds_tab", [P, G], U8)
+        nc.vector.memset(ds_tab[:].bitcast(I32), 0)
+        d_sc = tile("d_sc", [P, H], U8)
+        nc.gpsimd.memset(d_sc[:].bitcast(I32), 0)
+
+        offs_t = load_list("offs_t", offs)
+        two_t = load_list("two_t", two)
+        xs_rows = x_scales[0].bitcast(I32)
+        for quad in range(4):
+            nc.scalar.dma_start(
+                xs_tab[32 * quad : 32 * (quad + 1), :].bitcast(I32),
+                xs_rows[4 * quad : 4 * (quad + 1), :].unsqueeze(0).broadcast_to([8, 4, T // 4]),
+            )
+        w1_raw = [load_weight_half("w1_raw%d" % h, w1, h) for h in range(2)]
+        xw_tab = load_words("xw_tab", x_words)
+        kq_t = load_list("kq_t", kq)
+        ds_rows = d_scales[0].bitcast(I32).rearrange("(g e) c -> e g c", e=2)
+        for e in range(2):
+            nc.scalar.dma_start(ds_tab[e:P:16, :].bitcast(I32), ds_rows[e])
+        w2_raw = [load_weight_half("w2_raw%d" % h, w2, h) for h in range(2)]
+        nb_t = load_list("nb_t", nb)
+        gs_t = tile("gs_t", [P, PACK], F32)
+        nc.sync.dma_start(gs_t[:], gs.rearrange("(p t) o -> p (t o)", t=PACK))
+        dw_tab = load_words("dw_tab", d_words)
+
+        def gather(name, table, dtype, idx):
+            dst = tile(name, [P, S], dtype)
+            nc.vector.tensor_copy(dst[:], table[:].bitcast(dtype).indirect(idx[:]))
+            return dst
+
+        def cast_half(wb, raw, h):
+            nc.scalar.copy(
+                wb[:].rearrange("p (t m j) -> p m t j", t=PACK, j=PACK)[:, h * 64 : (h + 1) * 64],
+                raw[:].rearrange("p j (m t) -> p m t j", t=PACK),
+            )
+
+        def cast_half_pool(wb, raw, h):
+            nc.gpsimd.tensor_scalar(
+                wb[:].rearrange("p (t m j) -> p m t j", t=PACK, j=PACK)[:, h * 64 : (h + 1) * 64],
+                raw[:].rearrange("p j (m t) -> p m t j", t=PACK),
+                1.0,
+                0.0,
+                ALU.mult,
+                ALU.add,
+            )
+
+        def quantize(name, src, width):
+            codes = tile(name + "_codes", [P, width], U32)
+            scales = tile(name + "_scales", [P, width], U8)
+            nc.vector.quantize_mx(out=codes[:].bitcast(FP8X4), scales=scales[:], in_=src)
+            return codes, scales
+
+        def product(acc, lw, ls, t, rw, rs):
+            cols = slice(t * P, (t + 1) * P)
+            nc.tensor.matmul_mx(
+                out=acc,
+                lhsT=lw[:, cols].bitcast(FP8X4),
+                lhsT_scale=ls[:, cols],
+                rhs=rw[:].bitcast(FP8X4),
+                rhs_scale=rs[:],
+                start=True,
+                stop=True,
+            )
+
+        w1_bf = tile("w1_bf", [P, PACK * H], BF16)
+        w2_bf = tile("w2_bf", [P, PACK * H], BF16)
+        xq_s = gather("xq_s", xs_tab, U8, offs_t)
+        x2_s = gather("x2_s", xs_tab, U8, two_t)
+        for h in range(2):
+            cast_half(w1_bf, w1_raw[h], h)
+        w1_c, w1_s = quantize("w1", w1_bf[:], H)
+        xq_w = gather("xq_w", xw_tab, U32, offs_t)
+        x2_w = gather("x2_w", xw_tab, U32, two_t)
+
+        y_ps = [ps.tile([P, S], F32, name="y_ps%d" % t, tag="bank%d" % t) for t in range(PACK)]
+        c_ps = [ps.tile([P, S], F32, name="c_ps%d" % t) for t in range(PACK)]
+        for t in range(PACK):
+            product(y_ps[t][:], w1_c, w1_s, t, xq_w, xq_s)
+
+        y_win = [tile("y_win%d" % t, [P, S], F32) for t in range(PACK)]
+        y_own = [tile("y_own%d" % t, [P, S], F32) for t in range(PACK)]
+        e1 = [tile("e1_%d" % t, [P, S], F32) for t in range(PACK)]
+        t1 = [tile("t1_%d" % t, [P, S], F32) for t in range(PACK)]
+        vn = [tile("vn%d" % t, [P, S], F32) for t in range(PACK)]
+        q = [tile("q%d" % t, [P, S], F32) for t in range(PACK)]
+        vg = [tile("vg%d" % t, [P, S], F32) for t in range(PACK)]
+        halves = [slice(h * HALF, (h + 1) * HALF) for h in range(2)]
+        nb_half = [nb_t[:, h * HALF // 16 : (h + 1) * HALF // 16] for h in range(2)]
+
+        for h in range(2):
+            cast_half_pool(w2_bf, w2_raw[h], h)
+        dq_s = gather("dq_s", ds_tab, U8, kq_t)
+        for t in range(PACK):
+            nc.scalar.copy(y_win[t][:], y_ps[t][:])
+            nc.scalar.copy(y_own[t][:], y_ps[t][:])
+            for h in range(2):
+                nc.vector.tensor_tensor(e1[t][:, halves[h]], y_win[t][:].indirect(nb_half[h]), y_own[t][:, halves[h]], ALU.subtract)
+            if t == 1:
+                w2_c, w2_s = quantize("w2", w2_bf[:], H)
+                for u in range(PACK):
+                    product(c_ps[u][:], w2_c, w2_s, u, x2_w, x2_s)
+        for t in range(PACK):
+            nc.scalar.activation(t1[t][:], e1[t][:], ACT.Tanh, bias=bias0[:])
+            nc.vector.tensor_tensor(vn[t][:], c_ps[t][:], t1[t][:], ALU.add)
+        for t in range(PACK):
+            nc.vector.scalar_tensor_tensor(q[t][:], e1[t][:], -2.0, vn[t][:], ALU.mult, ALU.add)
+            nc.scalar.activation(vg[t][:], vn[t][:], ACT.Copy, scale=gs_t[:, t : t + 1])
+
+        dq_w = gather("dq_w", dw_tab, U32, kq_t)
+        for r in range(4):
+            src = 16 * (r // 2) + r % 2
+            nc.sync.dma_start(d_sc[r:P:32, :].bitcast(I32), dq_s[src:P:32, :].bitcast(I32))
+
+        out_v = out.rearrange("(m p) j -> p m j", p=P)
+        for h in range(2):
+            cols = halves[h]
+            planes = tile("planes%d" % h, [P, PACK, HALF], BF16)
+            e2 = [tile("e2_%d_%d" % (h, t), [P, HALF], F32) for t in range(PACK)]
+            t2 = [tile("t2_%d_%d" % (h, t), [P, HALF], F32) for t in range(PACK)]
+            for t in range(PACK):
+                nc.vector.tensor_tensor(e2[t][:], vn[t][:].indirect(nb_half[h]), q[t][:, cols], ALU.subtract)
+                nc.scalar.activation(t2[t][:], e2[t][:], ACT.Tanh, bias=bias0[:], scale=0.5)
+            for t in range(PACK):
+                nc.vector.scalar_tensor_tensor(planes[:, t, :], t2[t][:], gs_t[:, t : t + 1], vg[t][:, cols], ALU.mult, ALU.add)
+            z = tile("z%d" % h, [P, HALF, PACK], BF16)
+            if h == 0:
+                nc.scalar.copy(z[:], planes[:].rearrange("p t j -> p j t"))
+            else:
+                nc.vector.tensor_copy(z[:], planes[:].rearrange("p t j -> p j t"))
+            z_c, z_s = quantize("z%d" % h, z[:].rearrange("p j t -> p (j t)"), HALF)
+            for b in range(2):
+                acc = ps.tile([P, 2, HALF], F32, name="o_ps%d_%d" % (h, b), tag="bank%d" % (2 * h + b))
+                for u in range(2):
+                    product(acc[:, u, :], dq_w, d_sc, 2 * b + u, z_c, z_s)
+                res = tile("res%d_%d" % (h, b), [P, 2, HALF], F32)
+                if h == 1 and b == 1:
+                    nc.vector.tensor_scalar(res[:], acc[:], 0.0625, None, ALU.mult)
+                    nc.sync.dma_start(out_v[:, 2 * b : 2 * b + 2, cols], res[:])
+                else:
+                    nc.scalar.activation(res[:], acc[:], ACT.Copy, scale=0.0625)
+                    nc.sync.dma_start(out_v[:, 2 * b : 2 * b + 2, cols], res[:])

@@ -28,8 +28,8 @@ def tile_picked_symplec_none_p_kernel(
         sb = ctx.enter_context(tc.tile_pool(name="sb", bufs=1))
         ps = ctx.enter_context(tc.psum_pool(name="ps", bufs=1))
 
-        def tile(name, shape, dtype):
-            return sb.tile(shape, dtype, name=name, align_bytes=64)
+        def tile(name, shape, dtype, tag=None):
+            return sb.tile(shape, dtype, name=name, tag=tag or name, align_bytes=64)
 
         def load_list(name, src):
             dst = tile(name, [P, S // 16], U16)
@@ -55,47 +55,37 @@ def tile_picked_symplec_none_p_kernel(
         ds_tab = tile("ds_tab", [P, G], U8)
         nc.vector.memset(ds_tab[:].bitcast(I32), 0)
         d_sc = tile("d_sc", [P, H], U8)
-        nc.gpsimd.memset(d_sc[:].bitcast(I32), 0)
+        nc.vector.memset(d_sc[:].bitcast(I32), 0)
 
         offs_t = load_list("offs_t", offs)
         two_t = load_list("two_t", two)
         xs_rows = x_scales[0].bitcast(I32)
         for quad in range(4):
-            nc.scalar.dma_start(
+            nc.sync.dma_start(
                 xs_tab[32 * quad : 32 * (quad + 1), :].bitcast(I32),
                 xs_rows[4 * quad : 4 * (quad + 1), :].unsqueeze(0).broadcast_to([8, 4, T // 4]),
             )
-        w1_raw = [load_weight_half("w1_raw%d" % h, w1, h) for h in range(2)]
         xw_tab = load_words("xw_tab", x_words)
+        w1_raw = [load_weight_half("w1_raw%d" % h, w1, h) for h in range(2)]
         kq_t = load_list("kq_t", kq)
         ds_rows = d_scales[0].bitcast(I32).rearrange("(g e) c -> e g c", e=2)
         for e in range(2):
-            nc.scalar.dma_start(ds_tab[e:P:16, :].bitcast(I32), ds_rows[e])
-        w2_raw = [load_weight_half("w2_raw%d" % h, w2, h) for h in range(2)]
+            nc.sync.dma_start(ds_tab[e:P:16, :].bitcast(I32), ds_rows[e])
         nb_t = load_list("nb_t", nb)
+        w2_raw = [load_weight_half("w2_raw%d" % h, w2, h) for h in range(2)]
         gs_t = tile("gs_t", [P, PACK], F32)
         nc.sync.dma_start(gs_t[:], gs.rearrange("(p t) o -> p (t o)", t=PACK))
         dw_tab = load_words("dw_tab", d_words)
 
-        def gather(name, table, dtype, idx):
-            dst = tile(name, [P, S], dtype)
+        def gather(name, table, dtype, idx, tag=None):
+            dst = tile(name, [P, S], dtype, tag)
             nc.vector.tensor_copy(dst[:], table[:].bitcast(dtype).indirect(idx[:]))
             return dst
 
-        def cast_half(wb, raw, h):
-            nc.scalar.copy(
-                wb[:].rearrange("p (t m j) -> p m t j", t=PACK, j=PACK)[:, h * 64 : (h + 1) * 64],
-                raw[:].rearrange("p j (m t) -> p m t j", t=PACK),
-            )
-
-        def cast_half_pool(wb, raw, h):
-            nc.gpsimd.tensor_scalar(
-                wb[:].rearrange("p (t m j) -> p m t j", t=PACK, j=PACK)[:, h * 64 : (h + 1) * 64],
-                raw[:].rearrange("p j (m t) -> p m t j", t=PACK),
-                1.0,
-                0.0,
-                ALU.mult,
-                ALU.add,
+        def cast(copy, wb, raw, h, m0, m1):
+            copy(
+                wb[:].rearrange("p (t m j) -> p m t j", t=PACK, j=PACK)[:, h * 64 + m0 : h * 64 + m1],
+                raw[:].rearrange("p j (m t) -> p m t j", t=PACK)[:, m0:m1],
             )
 
         def quantize(name, src, width):
@@ -116,80 +106,89 @@ def tile_picked_symplec_none_p_kernel(
                 stop=True,
             )
 
-        w1_bf = tile("w1_bf", [P, PACK * H], BF16)
-        w2_bf = tile("w2_bf", [P, PACK * H], BF16)
+        w1_bf = tile("w1_bf", [P, PACK * H], BF16, "w_bf")
         xq_s = gather("xq_s", xs_tab, U8, offs_t)
         x2_s = gather("x2_s", xs_tab, U8, two_t)
-        for h in range(2):
-            cast_half(w1_bf, w1_raw[h], h)
-        w1_c, w1_s = quantize("w1", w1_bf[:], H)
         xq_w = gather("xq_w", xw_tab, U32, offs_t)
-        x2_w = gather("x2_w", xw_tab, U32, two_t)
+        x2_w = gather("x2_w", xw_tab, U32, two_t, "late_words")
+        cast(nc.scalar.copy, w1_bf, w1_raw[0], 0, 0, 64)
+        cast(nc.scalar.copy, w1_bf, w1_raw[1], 1, 0, 32)
+        cast(nc.vector.tensor_copy, w1_bf, w1_raw[1], 1, 32, 64)
+        w1_c, w1_s = quantize("w1", w1_bf[:], H)
+        dq_s = gather("dq_s", ds_tab, U8, kq_t)
+        w2_bf = tile("w2_bf", [P, PACK * H], BF16, "w_bf")
+        cast(nc.scalar.copy, w2_bf, w2_raw[0], 0, 0, 64)
+        cast(nc.vector.tensor_copy, w2_bf, w2_raw[1], 1, 0, 64)
 
         y_ps = [ps.tile([P, S], F32, name="y_ps%d" % t, tag="bank%d" % t) for t in range(PACK)]
         c_ps = [ps.tile([P, S], F32, name="c_ps%d" % t) for t in range(PACK)]
         for t in range(PACK):
             product(y_ps[t][:], w1_c, w1_s, t, xq_w, xq_s)
 
-        y_win = [tile("y_win%d" % t, [P, S], F32) for t in range(PACK)]
-        y_own = [tile("y_own%d" % t, [P, S], F32) for t in range(PACK)]
+        y_pair = [tile("y_pair%d" % t, [P, 2 * S], F32) for t in range(PACK)]
+        v_pair = [tile("v_pair%d" % t, [P, 2 * S], F32) for t in range(PACK)]
+        y_last = tile("y_last", [P, S], F32)
+        q_last = tile("q_last", [P, S], F32)
+        nc.vector.memset(y_pair[0][:, S:], 0.0)
+        nc.vector.memset(v_pair[0][:, S:], 0.0)
+        y_own = [y_pair[t + 1][:, S:] for t in range(PACK - 1)] + [y_last[:]]
+        q = [v_pair[t + 1][:, S:] for t in range(PACK - 1)] + [q_last[:]]
+        vn = [v_pair[t][:, :S] for t in range(PACK)]
         e1 = [tile("e1_%d" % t, [P, S], F32) for t in range(PACK)]
         t1 = [tile("t1_%d" % t, [P, S], F32) for t in range(PACK)]
-        vn = [tile("vn%d" % t, [P, S], F32) for t in range(PACK)]
-        q = [tile("q%d" % t, [P, S], F32) for t in range(PACK)]
         vg = [tile("vg%d" % t, [P, S], F32) for t in range(PACK)]
-        halves = [slice(h * HALF, (h + 1) * HALF) for h in range(2)]
-        nb_half = [nb_t[:, h * HALF // 16 : (h + 1) * HALF // 16] for h in range(2)]
 
-        for h in range(2):
-            cast_half_pool(w2_bf, w2_raw[h], h)
-        dq_s = gather("dq_s", ds_tab, U8, kq_t)
         for t in range(PACK):
-            nc.scalar.copy(y_win[t][:], y_ps[t][:])
-            nc.scalar.copy(y_own[t][:], y_ps[t][:])
-            for h in range(2):
-                nc.vector.tensor_tensor(e1[t][:, halves[h]], y_win[t][:].indirect(nb_half[h]), y_own[t][:, halves[h]], ALU.subtract)
-            if t == 1:
+            nc.scalar.copy(y_pair[t][:, :S], y_ps[t][:])
+            nc.scalar.copy(y_own[t], y_ps[t][:])
+            nc.vector.tensor_tensor(e1[t][:], y_pair[t][:].indirect(nb_t[:]), y_own[t], ALU.subtract)
+            if t == 0:
                 w2_c, w2_s = quantize("w2", w2_bf[:], H)
-                for u in range(PACK):
-                    product(c_ps[u][:], w2_c, w2_s, u, x2_w, x2_s)
+        for t in range(PACK):
+            product(c_ps[t][:], w2_c, w2_s, t, x2_w, x2_s)
         for t in range(PACK):
             nc.scalar.activation(t1[t][:], e1[t][:], ACT.Tanh, bias=bias0[:])
-            nc.vector.tensor_tensor(vn[t][:], c_ps[t][:], t1[t][:], ALU.add)
+            nc.vector.tensor_tensor(vn[t], c_ps[t][:], t1[t][:], ALU.add)
         for t in range(PACK):
-            nc.vector.scalar_tensor_tensor(q[t][:], e1[t][:], -2.0, vn[t][:], ALU.mult, ALU.add)
-            nc.scalar.activation(vg[t][:], vn[t][:], ACT.Copy, scale=gs_t[:, t : t + 1])
+            nc.vector.scalar_tensor_tensor(q[t], e1[t][:], -2.0, vn[t], ALU.mult, ALU.add)
+            nc.scalar.activation(vg[t][:], vn[t], ACT.Copy, scale=gs_t[:, t : t + 1])
 
-        dq_w = gather("dq_w", dw_tab, U32, kq_t)
+        dq_w = gather("dq_w", dw_tab, U32, kq_t, "late_words")
         for r in range(4):
             src = 16 * (r // 2) + r % 2
             nc.sync.dma_start(d_sc[r:P:32, :].bitcast(I32), dq_s[src:P:32, :].bitcast(I32))
 
         out_v = out.rearrange("(m p) j -> p m j", p=P)
-        for h in range(2):
-            cols = halves[h]
-            planes = tile("planes%d" % h, [P, PACK, HALF], BF16)
-            e2 = [tile("e2_%d_%d" % (h, t), [P, HALF], F32) for t in range(PACK)]
-            t2 = [tile("t2_%d_%d" % (h, t), [P, HALF], F32) for t in range(PACK)]
+        pieces = [(0, 256), (256, 256)]
+        for n, (j0, width) in enumerate(pieces):
+            final = n == len(pieces) - 1
+            cols = slice(j0, j0 + width)
+            nb_piece = nb_t[:, j0 // 16 : (j0 + width) // 16]
+            planes = tile("planes%d" % n, [P, PACK, width], BF16)
+            e2 = [tile("e2_%d_%d" % (n, t), [P, width], F32) for t in range(PACK)]
+            t2 = [tile("t2_%d_%d" % (n, t), [P, width], F32) for t in range(PACK)]
             for t in range(PACK):
-                nc.vector.tensor_tensor(e2[t][:], vn[t][:].indirect(nb_half[h]), q[t][:, cols], ALU.subtract)
+                nc.vector.tensor_tensor(e2[t][:], v_pair[t][:].indirect(nb_piece), q[t][:, cols], ALU.subtract)
                 nc.scalar.activation(t2[t][:], e2[t][:], ACT.Tanh, bias=bias0[:], scale=0.5)
             for t in range(PACK):
                 nc.vector.scalar_tensor_tensor(planes[:, t, :], t2[t][:], gs_t[:, t : t + 1], vg[t][:, cols], ALU.mult, ALU.add)
-            z = tile("z%d" % h, [P, HALF, PACK], BF16)
-            if h == 0:
-                nc.scalar.copy(z[:], planes[:].rearrange("p t j -> p j t"))
-            else:
+            z = tile("z%d" % n, [P, width, PACK], BF16)
+            if final:
                 nc.vector.tensor_copy(z[:], planes[:].rearrange("p t j -> p j t"))
-            z_c, z_s = quantize("z%d" % h, z[:].rearrange("p j t -> p (j t)"), HALF)
+            else:
+                nc.scalar.copy(z[:], planes[:].rearrange("p t j -> p j t"))
+            z_c, z_s = quantize("z%d" % n, z[:].rearrange("p j t -> p (j t)"), width)
             for b in range(2):
-                acc = ps.tile([P, 2, HALF], F32, name="o_ps%d_%d" % (h, b), tag="bank%d" % (2 * h + b))
+                acc = ps.tile([P, 2, width], F32, name="o_ps%d_%d" % (n, b), tag="bank%d" % ((2 * n + b) % 4))
                 for u in range(2):
                     product(acc[:, u, :], dq_w, d_sc, 2 * b + u, z_c, z_s)
-                res = tile("res%d_%d" % (h, b), [P, 2, HALF], F32)
-                if h == 1 and b == 1:
+                res = tile("res%d_%d" % (n, b), [P, 2, width], F32)
+                if final and b == 1:
                     nc.vector.tensor_scalar(res[:], acc[:], 0.0625, None, ALU.mult)
                     nc.sync.dma_start(out_v[:, 2 * b : 2 * b + 2, cols], res[:])
+                elif final:
+                    nc.scalar.activation(res[:], acc[:], ACT.Copy, scale=0.0625)
+                    nc.scalar.dma_start(out_v[:, 2 * b : 2 * b + 2, cols], res[:])
                 else:
                     nc.scalar.activation(res[:], acc[:], ACT.Copy, scale=0.0625)
                     nc.sync.dma_start(out_v[:, 2 * b : 2 * b + 2, cols], res[:])

@@ -18,6 +18,7 @@ ALU = mybir.AluOpType
 P = 128
 PACK = 4
 HALF = S // 2
+NPOOL = 0
 
 
 def tile_picked_symplec_none_p_kernel(
@@ -117,76 +118,77 @@ def tile_picked_symplec_none_p_kernel(
         w1_c, w1_s = quantize("w1", w1_bf[:], H)
         dq_s = gather("dq_s", ds_tab, U8, kq_t)
         w2_bf = tile("w2_bf", [P, PACK * H], BF16, "w_bf")
-        cast(nc.scalar.copy, w2_bf, w2_raw[0], 0, 0, 64)
-        cast(nc.vector.tensor_copy, w2_bf, w2_raw[1], 1, 0, 64)
 
         y_ps = [ps.tile([P, S], F32, name="y_ps%d" % t, tag="bank%d" % t) for t in range(PACK)]
         c_ps = [ps.tile([P, S], F32, name="c_ps%d" % t) for t in range(PACK)]
         for t in range(PACK):
             product(y_ps[t][:], w1_c, w1_s, t, xq_w, xq_s)
 
-        y_pair = [tile("y_pair%d" % t, [P, 2 * S], F32) for t in range(PACK)]
-        v_pair = [tile("v_pair%d" % t, [P, 2 * S], F32) for t in range(PACK)]
-        y_last = tile("y_last", [P, S], F32)
-        q_last = tile("q_last", [P, S], F32)
-        nc.vector.memset(y_pair[0][:, S:], 0.0)
-        nc.vector.memset(v_pair[0][:, S:], 0.0)
-        y_own = [y_pair[t + 1][:, S:] for t in range(PACK - 1)] + [y_last[:]]
-        q = [v_pair[t + 1][:, S:] for t in range(PACK - 1)] + [q_last[:]]
-        vn = [v_pair[t][:, :S] for t in range(PACK)]
-        e1 = [tile("e1_%d" % t, [P, S], F32) for t in range(PACK)]
-        t1 = [tile("t1_%d" % t, [P, S], F32) for t in range(PACK)]
-        vg = [tile("vg%d" % t, [P, S], F32) for t in range(PACK)]
+        def plane_tiles(name, width):
+            return [tile("%s%d" % (name, t), [P, width], F32) for t in range(PACK)]
+
+        y2, g1, d1, t1, vn, x2 = (plane_tiles(name, S) for name in ("y2_", "g1_", "d1_", "t1_", "vn_", "x2_"))
+        halves = [slice(h * HALF, (h + 1) * HALF) for h in range(2)]
+        nb_half = [nb_t[:, h * HALF // 16 : (h + 1) * HALF // 16] for h in range(2)]
 
         for t in range(PACK):
-            nc.scalar.copy(y_pair[t][:, :S], y_ps[t][:])
-            nc.scalar.copy(y_own[t], y_ps[t][:])
-            nc.vector.tensor_tensor(e1[t][:], y_pair[t][:].indirect(nb_t[:]), y_own[t], ALU.subtract)
-            if t == 0:
-                w2_c, w2_s = quantize("w2", w2_bf[:], H)
+            nc.scalar.activation(y2[t][:], y_ps[t][:], ACT.Copy, scale=2.0)
+            cast(nc.scalar.copy, w2_bf, w2_raw[t // 2], t // 2, 32 * (t % 2), 32 * (t % 2 + 1))
+            for h in range(2):
+                nc.vector.tensor_copy(g1[t][:, halves[h]], y2[t][:].indirect(nb_half[h]))
+            nc.gpsimd.tensor_tensor(d1[t][:], y2[t][:], g1[t][:], ALU.subtract)
+        w2_c, w2_s = quantize("w2", w2_bf[:], H)
         for t in range(PACK):
             product(c_ps[t][:], w2_c, w2_s, t, x2_w, x2_s)
         for t in range(PACK):
-            nc.scalar.activation(t1[t][:], e1[t][:], ACT.Tanh, bias=bias0[:])
-            nc.vector.tensor_tensor(vn[t], c_ps[t][:], t1[t][:], ALU.add)
-        for t in range(PACK):
-            nc.vector.scalar_tensor_tensor(q[t], e1[t][:], -2.0, vn[t], ALU.mult, ALU.add)
-            nc.scalar.activation(vg[t][:], vn[t], ACT.Copy, scale=gs_t[:, t : t + 1])
-
+            nc.scalar.activation(t1[t][:], d1[t][:], ACT.Tanh, bias=bias0[:], scale=0.5)
         dq_w = gather("dq_w", dw_tab, U32, kq_t, "late_words")
         for r in range(4):
             src = 16 * (r // 2) + r % 2
             nc.sync.dma_start(d_sc[r:P:32, :].bitcast(I32), dq_s[src:P:32, :].bitcast(I32))
 
-        out_v = out.rearrange("(m p) j -> p m j", p=P)
-        pieces = [(0, 256), (256, 256)]
-        for n, (j0, width) in enumerate(pieces):
-            final = n == len(pieces) - 1
-            cols = slice(j0, j0 + width)
-            nb_piece = nb_t[:, j0 // 16 : (j0 + width) // 16]
-            planes = tile("planes%d" % n, [P, PACK, width], BF16)
-            e2 = [tile("e2_%d_%d" % (n, t), [P, width], F32) for t in range(PACK)]
-            t2 = [tile("t2_%d_%d" % (n, t), [P, width], F32) for t in range(PACK)]
-            for t in range(PACK):
-                nc.vector.tensor_tensor(e2[t][:], v_pair[t][:].indirect(nb_piece), q[t][:, cols], ALU.subtract)
-                nc.scalar.activation(t2[t][:], e2[t][:], ACT.Tanh, bias=bias0[:], scale=0.5)
-            for t in range(PACK):
-                nc.vector.scalar_tensor_tensor(planes[:, t, :], t2[t][:], gs_t[:, t : t + 1], vg[t][:, cols], ALU.mult, ALU.add)
-            z = tile("z%d" % n, [P, width, PACK], BF16)
-            if final:
-                nc.vector.tensor_copy(z[:], planes[:].rearrange("p t j -> p j t"))
+        planes = [tile("planes%d" % h, [P, PACK, HALF], BF16) for h in range(2)]
+        g2, d2, t2, u2 = (plane_tiles(name, HALF) for name in ("g2_", "d2_", "t2_", "u2_"))
+        x2_own, vg, e2, t2n = (plane_tiles(name, HALF) for name in ("x2_own", "vg_", "e2_", "t2n_"))
+        first, second = halves
+        for t in range(PACK):
+            nc.vector.tensor_tensor(vn[t][:], c_ps[t][:], t1[t][:], ALU.subtract)
+            if t < NPOOL:
+                nc.gpsimd.tensor_tensor(x2[t][:], y2[t][:], vn[t][:], ALU.add)
             else:
-                nc.scalar.copy(z[:], planes[:].rearrange("p t j -> p j t"))
-            z_c, z_s = quantize("z%d" % n, z[:].rearrange("p j t -> p (j t)"), width)
+                nc.vector.scalar_tensor_tensor(x2[t][:], y_ps[t][:], 2.0, vn[t][:], ALU.mult, ALU.add)
+        for t in range(PACK):
+            nc.vector.tensor_copy(g2[t][:], x2[t][:].indirect(nb_half[0]))
+            nc.gpsimd.tensor_tensor(d2[t][:], x2[t][:, first], g2[t][:], ALU.subtract)
+            nc.scalar.activation(t2[t][:], d2[t][:], ACT.Tanh, bias=bias0[:], scale=0.5)
+            nc.gpsimd.tensor_tensor(u2[t][:], vn[t][:, first], t2[t][:], ALU.subtract)
+            nc.scalar.activation(planes[0][:, t, :], u2[t][:], ACT.Copy, scale=gs_t[:, t : t + 1])
+            nc.scalar.copy(x2_own[t][:], x2[t][:, second])
+            nc.scalar.activation(vg[t][:], vn[t][:, second], ACT.Copy, scale=gs_t[:, t : t + 1])
+        for t in range(PACK):
+            nc.vector.tensor_tensor(e2[t][:], x2[t][:].indirect(nb_half[1]), x2_own[t][:], ALU.subtract)
+            nc.scalar.activation(t2n[t][:], e2[t][:], ACT.Tanh, bias=bias0[:], scale=0.5)
+        for t in range(PACK):
+            nc.vector.scalar_tensor_tensor(planes[1][:, t, :], t2n[t][:], gs_t[:, t : t + 1], vg[t][:], ALU.mult, ALU.add)
+
+        out_v = out.rearrange("(m p) j -> p m j", p=P)
+        for h in range(2):
+            cols = halves[h]
+            z = tile("z%d" % h, [P, HALF, PACK], BF16)
+            if h == 1:
+                nc.vector.tensor_copy(z[:], planes[h][:].rearrange("p t j -> p j t"))
+            else:
+                nc.scalar.copy(z[:], planes[h][:].rearrange("p t j -> p j t"))
+            z_c, z_s = quantize("z%d" % h, z[:].rearrange("p j t -> p (j t)"), HALF)
             for b in range(2):
-                acc = ps.tile([P, 2, width], F32, name="o_ps%d_%d" % (n, b), tag="bank%d" % ((2 * n + b) % 4))
+                acc = ps.tile([P, 2, HALF], F32, name="o_ps%d_%d" % (h, b), tag="bank%d" % (2 * h + b))
                 for u in range(2):
                     product(acc[:, u, :], dq_w, d_sc, 2 * b + u, z_c, z_s)
-                res = tile("res%d_%d" % (n, b), [P, 2, width], F32)
-                if final and b == 1:
+                res = tile("res%d_%d" % (h, b), [P, 2, HALF], F32)
+                if h == 1 and b == 1:
                     nc.vector.tensor_scalar(res[:], acc[:], 0.0625, None, ALU.mult)
                     nc.sync.dma_start(out_v[:, 2 * b : 2 * b + 2, cols], res[:])
-                elif final:
+                elif h == 1:
                     nc.scalar.activation(res[:], acc[:], ACT.Copy, scale=0.0625)
                     nc.scalar.dma_start(out_v[:, 2 * b : 2 * b + 2, cols], res[:])
                 else:

@@ -17,8 +17,11 @@ ALU = mybir.AluOpType
 
 P = 128
 PACK = 4
+QUADRANT = 32
+GROUP = 16
 HALF = S // 2
-NPOOL = 0
+DEALT = P // 2
+OUT_SCALE = 0.0625
 
 
 def tile_picked_symplec_none_p_kernel(
@@ -32,8 +35,11 @@ def tile_picked_symplec_none_p_kernel(
         def tile(name, shape, dtype, tag=None):
             return sb.tile(shape, dtype, name=name, tag=tag or name, align_bytes=64)
 
+        def feature_tiles(name):
+            return [tile("%s%d" % (name, t), [P, S], F32) for t in range(PACK)]
+
         def load_list(name, src):
-            dst = tile(name, [P, S // 16], U16)
+            dst = tile(name, [P, S // GROUP], U16)
             nc.sync.dma_start(dst[:], src)
             return dst
 
@@ -47,45 +53,14 @@ def tile_picked_symplec_none_p_kernel(
             nc.sync.dma_start(dst[:], src.rearrange("(p j) c -> p j c", j=PACK)[:, :, h * HALF : (h + 1) * HALF])
             return dst
 
-        zero = tile("zero", [P, 1], F32)
-        nc.vector.memset(zero[:], 0.0)
-        bias0 = tile("bias0", [P, 1], F32)
-        nc.scalar.activation(bias0[:], zero[:], ACT.Tanh)
-
-        xs_tab = tile("xs_tab", [P, T], U8)
-        ds_tab = tile("ds_tab", [P, G], U8)
-        nc.vector.memset(ds_tab[:].bitcast(I32), 0)
-        d_sc = tile("d_sc", [P, H], U8)
-        nc.vector.memset(d_sc[:].bitcast(I32), 0)
-
-        offs_t = load_list("offs_t", offs)
-        two_t = load_list("two_t", two)
-        xs_rows = x_scales[0].bitcast(I32)
-        for quad in range(4):
-            nc.sync.dma_start(
-                xs_tab[32 * quad : 32 * (quad + 1), :].bitcast(I32),
-                xs_rows[4 * quad : 4 * (quad + 1), :].unsqueeze(0).broadcast_to([8, 4, T // 4]),
-            )
-        xw_tab = load_words("xw_tab", x_words)
-        w1_raw = [load_weight_half("w1_raw%d" % h, w1, h) for h in range(2)]
-        kq_t = load_list("kq_t", kq)
-        ds_rows = d_scales[0].bitcast(I32).rearrange("(g e) c -> e g c", e=2)
-        for e in range(2):
-            nc.sync.dma_start(ds_tab[e:P:16, :].bitcast(I32), ds_rows[e])
-        nb_t = load_list("nb_t", nb)
-        w2_raw = [load_weight_half("w2_raw%d" % h, w2, h) for h in range(2)]
-        gs_t = tile("gs_t", [P, PACK], F32)
-        nc.sync.dma_start(gs_t[:], gs.rearrange("(p t) o -> p (t o)", t=PACK))
-        dw_tab = load_words("dw_tab", d_words)
-
-        def gather(name, table, dtype, idx, tag=None):
+        def gather_packed(name, table, dtype, idx, tag=None):
             dst = tile(name, [P, S], dtype, tag)
             nc.vector.tensor_copy(dst[:], table[:].bitcast(dtype).indirect(idx[:]))
             return dst
 
-        def cast(copy, wb, raw, h, m0, m1):
+        def cast(copy, dealt, raw, h, m0, m1):
             copy(
-                wb[:].rearrange("p (t m j) -> p m t j", t=PACK, j=PACK)[:, h * 64 + m0 : h * 64 + m1],
+                dealt[:].rearrange("p (t m j) -> p m t j", t=PACK, j=PACK)[:, h * DEALT + m0 : h * DEALT + m1],
                 raw[:].rearrange("p j (m t) -> p m t j", t=PACK)[:, m0:m1],
             )
 
@@ -95,102 +70,150 @@ def tile_picked_symplec_none_p_kernel(
             nc.vector.quantize_mx(out=codes[:].bitcast(FP8X4), scales=scales[:], in_=src)
             return codes, scales
 
-        def product(acc, lw, ls, t, rw, rs):
-            cols = slice(t * P, (t + 1) * P)
+        def product(acc, lhs_words, lhs_scales, block, rhs_words, rhs_scales):
+            cols = slice(block * P, (block + 1) * P)
             nc.tensor.matmul_mx(
                 out=acc,
-                lhsT=lw[:, cols].bitcast(FP8X4),
-                lhsT_scale=ls[:, cols],
-                rhs=rw[:].bitcast(FP8X4),
-                rhs_scale=rs[:],
+                lhsT=lhs_words[:, cols].bitcast(FP8X4),
+                lhsT_scale=lhs_scales[:, cols],
+                rhs=rhs_words[:].bitcast(FP8X4),
+                rhs_scale=rhs_scales[:],
                 start=True,
                 stop=True,
             )
 
-        w1_bf = tile("w1_bf", [P, PACK * H], BF16, "w_bf")
-        xq_s = gather("xq_s", xs_tab, U8, offs_t)
-        x2_s = gather("x2_s", xs_tab, U8, two_t)
-        xq_w = gather("xq_w", xw_tab, U32, offs_t)
-        x2_w = gather("x2_w", xw_tab, U32, two_t, "late_words")
-        cast(nc.scalar.copy, w1_bf, w1_raw[0], 0, 0, 64)
-        cast(nc.scalar.copy, w1_bf, w1_raw[1], 1, 0, 32)
-        cast(nc.vector.tensor_copy, w1_bf, w1_raw[1], 1, 32, 64)
-        w1_c, w1_s = quantize("w1", w1_bf[:], H)
-        dq_s = gather("dq_s", ds_tab, U8, kq_t)
-        w2_bf = tile("w2_bf", [P, PACK * H], BF16, "w_bf")
+        zero = tile("zero", [P, 1], F32)
+        nc.vector.memset(zero[:], 0.0)
+        zero_bias = tile("zero_bias", [P, 1], F32)
+        nc.scalar.activation(zero_bias[:], zero[:], ACT.Tanh)
+
+        xs_table = tile("xs_table", [P, T], U8)
+        ds_table = tile("ds_table", [P, G], U8)
+        nc.vector.memset(ds_table[:].bitcast(I32), 0)
+        d_plane = tile("d_plane", [P, H], U8)
+        nc.vector.memset(d_plane[:].bitcast(I32), 0)
+
+        offs_t = load_list("offs_t", offs)
+        xs_rows = x_scales[0].bitcast(I32)
+        for quad in range(P // QUADRANT):
+            nc.sync.dma_start(
+                xs_table[QUADRANT * quad : QUADRANT * (quad + 1), :].bitcast(I32),
+                xs_rows[4 * quad : 4 * (quad + 1), :].unsqueeze(0).broadcast_to([QUADRANT // 4, 4, T // 4]),
+            )
+        two_t = load_list("two_t", two)
+        xw_table = load_words("xw_table", x_words)
+        w1_raw = [load_weight_half("w1_raw%d" % h, w1, h) for h in range(2)]
+        kq_t = load_list("kq_t", kq)
+        ds_rows = d_scales[0].bitcast(I32).rearrange("(g e) c -> e g c", e=2)
+        for e in range(2):
+            nc.sync.dma_start(ds_table[e:P:GROUP, :].bitcast(I32), ds_rows[e])
+        nb_t = load_list("nb_t", nb)
+        w2_raw = [load_weight_half("w2_raw%d" % h, w2, h) for h in range(2)]
+        gs_t = tile("gs_t", [P, PACK], F32)
+        nc.sync.dma_start(gs_t[:], gs.rearrange("(p t) o -> p (t o)", t=PACK))
+        dw_table = load_words("dw_table", d_words)
+
+        w1_dealt = tile("w1_dealt", [P, PACK * H], BF16, "dealt")
+        xq_scales = gather_packed("xq_scales", xs_table, U8, offs_t)
+        x2_scales = gather_packed("x2_scales", xs_table, U8, two_t)
+        xq_words = gather_packed("xq_words", xw_table, U32, offs_t)
+        x2_words = gather_packed("x2_words", xw_table, U32, two_t, "picked_words")
+        cast(nc.scalar.copy, w1_dealt, w1_raw[0], 0, 0, DEALT)
+        cast(nc.scalar.copy, w1_dealt, w1_raw[1], 1, 0, DEALT // 2)
+        cast(nc.vector.tensor_copy, w1_dealt, w1_raw[1], 1, DEALT // 2, DEALT)
+        w1_codes, w1_scales = quantize("w1", w1_dealt[:], H)
+        dq_scales = gather_packed("dq_scales", ds_table, U8, kq_t)
+        w2_dealt = tile("w2_dealt", [P, PACK * H], BF16, "dealt")
+        cast(nc.scalar.copy, w2_dealt, w2_raw[0], 0, 0, DEALT)
+        cast(nc.vector.tensor_copy, w2_dealt, w2_raw[1], 1, 0, DEALT)
 
         y_ps = [ps.tile([P, S], F32, name="y_ps%d" % t, tag="bank%d" % t) for t in range(PACK)]
         c_ps = [ps.tile([P, S], F32, name="c_ps%d" % t) for t in range(PACK)]
         for t in range(PACK):
-            product(y_ps[t][:], w1_c, w1_s, t, xq_w, xq_s)
+            product(y_ps[t][:], w1_codes, w1_scales, t, xq_words, xq_scales)
 
-        def plane_tiles(name, width):
-            return [tile("%s%d" % (name, t), [P, width], F32) for t in range(PACK)]
-
-        y2, g1, d1, t1, vn, x2 = (plane_tiles(name, S) for name in ("y2_", "g1_", "d1_", "t1_", "vn_", "x2_"))
+        y_window = [tile("y_window%d" % t, [P, S if t == 0 else 2 * S], F32) for t in range(PACK)]
+        y_last = tile("y_last", [P, S], F32)
+        y_own = [y_window[t + 1][:, S:] for t in range(PACK - 1)] + [y_last[:]]
+        dy, tanh_dy, vn, bracket, gs_vn = (feature_tiles(name) for name in ("dy", "tanh_dy", "vn", "bracket", "gs_vn"))
         halves = [slice(h * HALF, (h + 1) * HALF) for h in range(2)]
-        nb_half = [nb_t[:, h * HALF // 16 : (h + 1) * HALF // 16] for h in range(2)]
+        nb_half = [nb_t[:, h * HALF // GROUP : (h + 1) * HALF // GROUP] for h in range(2)]
+
+        nc.scalar.copy(y_window[0][:], y_ps[0][:])
+        for h in range(2):
+            nc.scalar.copy(y_own[0][:, halves[h]], y_ps[0][:, halves[h]])
+            nc.vector.tensor_tensor(
+                dy[0][:, halves[h]], y_window[0][:].indirect(nb_half[h]), y_own[0][:, halves[h]], ALU.subtract
+            )
+        w2_codes, w2_scales = quantize("w2", w2_dealt[:], H)
+        for t in range(1, PACK):
+            nc.scalar.copy(y_window[t][:, :S], y_ps[t][:])
+            nc.scalar.copy(y_own[t], y_ps[t][:])
+            nc.vector.tensor_tensor(dy[t][:], y_window[t][:].indirect(nb_t[:]), y_own[t], ALU.subtract)
+        for t in range(PACK):
+            product(c_ps[t][:], w2_codes, w2_scales, t, x2_words, x2_scales)
 
         for t in range(PACK):
-            nc.scalar.activation(y2[t][:], y_ps[t][:], ACT.Copy, scale=2.0)
-            cast(nc.scalar.copy, w2_bf, w2_raw[t // 2], t // 2, 32 * (t % 2), 32 * (t % 2 + 1))
-            for h in range(2):
-                nc.vector.tensor_copy(g1[t][:, halves[h]], y2[t][:].indirect(nb_half[h]))
-            nc.gpsimd.tensor_tensor(d1[t][:], y2[t][:], g1[t][:], ALU.subtract)
-        w2_c, w2_s = quantize("w2", w2_bf[:], H)
+            nc.scalar.activation(tanh_dy[t][:], dy[t][:], ACT.Tanh, bias=zero_bias[:])
+            nc.vector.tensor_tensor(vn[t][:], c_ps[t][:], tanh_dy[t][:], ALU.add)
         for t in range(PACK):
-            product(c_ps[t][:], w2_c, w2_s, t, x2_w, x2_s)
-        for t in range(PACK):
-            nc.scalar.activation(t1[t][:], d1[t][:], ACT.Tanh, bias=bias0[:], scale=0.5)
-        dq_w = gather("dq_w", dw_tab, U32, kq_t, "late_words")
+            nc.vector.scalar_tensor_tensor(bracket[t][:], dy[t][:], -2.0, vn[t][:], ALU.mult, ALU.add)
+            nc.scalar.activation(gs_vn[t][:], vn[t][:], ACT.Copy, scale=gs_t[:, t : t + 1])
+
+        dq_words = gather_packed("dq_words", dw_table, U32, kq_t, "picked_words")
         for r in range(4):
-            src = 16 * (r // 2) + r % 2
-            nc.sync.dma_start(d_sc[r:P:32, :].bitcast(I32), dq_s[src:P:32, :].bitcast(I32))
+            src = GROUP * (r // 2) + r % 2
+            nc.sync.dma_start(d_plane[r:P:QUADRANT, :].bitcast(I32), dq_scales[src:P:QUADRANT, :].bitcast(I32))
 
-        planes = [tile("planes%d" % h, [P, PACK, HALF], BF16) for h in range(2)]
-        g2, d2, t2, u2 = (plane_tiles(name, HALF) for name in ("g2_", "d2_", "t2_", "u2_"))
-        x2_own, vg, e2, t2n = (plane_tiles(name, HALF) for name in ("x2_own", "vg_", "e2_", "t2n_"))
-        first, second = halves
-        for t in range(PACK):
-            nc.vector.tensor_tensor(vn[t][:], c_ps[t][:], t1[t][:], ALU.subtract)
-            if t < NPOOL:
-                nc.gpsimd.tensor_tensor(x2[t][:], y2[t][:], vn[t][:], ALU.add)
-            else:
-                nc.vector.scalar_tensor_tensor(x2[t][:], y_ps[t][:], 2.0, vn[t][:], ALU.mult, ALU.add)
-        for t in range(PACK):
-            nc.vector.tensor_copy(g2[t][:], x2[t][:].indirect(nb_half[0]))
-            nc.gpsimd.tensor_tensor(d2[t][:], x2[t][:, first], g2[t][:], ALU.subtract)
-            nc.scalar.activation(t2[t][:], d2[t][:], ACT.Tanh, bias=bias0[:], scale=0.5)
-            nc.gpsimd.tensor_tensor(u2[t][:], vn[t][:, first], t2[t][:], ALU.subtract)
-            nc.scalar.activation(planes[0][:, t, :], u2[t][:], ACT.Copy, scale=gs_t[:, t : t + 1])
-            nc.scalar.copy(x2_own[t][:], x2[t][:, second])
-            nc.scalar.activation(vg[t][:], vn[t][:, second], ACT.Copy, scale=gs_t[:, t : t + 1])
-        for t in range(PACK):
-            nc.vector.tensor_tensor(e2[t][:], x2[t][:].indirect(nb_half[1]), x2_own[t][:], ALU.subtract)
-            nc.scalar.activation(t2n[t][:], e2[t][:], ACT.Tanh, bias=bias0[:], scale=0.5)
-        for t in range(PACK):
-            nc.vector.scalar_tensor_tensor(planes[1][:, t, :], t2n[t][:], gs_t[:, t : t + 1], vg[t][:], ALU.mult, ALU.add)
+        def second_lookup(h, dx, tanh_dx):
+            for t in range(PACK):
+                nc.vector.tensor_tensor(dx[:, t, :], vn[t][:].indirect(nb_half[h]), bracket[t][:, halves[h]], ALU.subtract)
+                nc.scalar.activation(tanh_dx[:, t, :], dx[:, t, :], ACT.Tanh, bias=zero_bias[:], scale=0.5)
+
+        def make_z(h, tanh_dx):
+            z = tile("z%d" % h, [P, PACK, HALF], BF16)
+            for t in range(PACK):
+                nc.vector.scalar_tensor_tensor(
+                    z[:, t, :], tanh_dx[:, t, :], gs_t[:, t : t + 1], gs_vn[t][:, halves[h]], ALU.mult, ALU.add
+                )
+            return z
+
+        def quantize_z(name, z, j0, j1, copy):
+            grouped = tile(name, [P, j1 - j0, PACK], BF16)
+            copy(grouped[:], z[:, :, j0:j1].rearrange("p t j -> p j t"))
+            return quantize(name, grouped[:].rearrange("p j t -> p (j t)"), j1 - j0)
 
         out_v = out.rearrange("(m p) j -> p m j", p=P)
-        for h in range(2):
-            cols = halves[h]
-            z = tile("z%d" % h, [P, HALF, PACK], BF16)
-            if h == 1:
-                nc.vector.tensor_copy(z[:], planes[h][:].rearrange("p t j -> p j t"))
-            else:
-                nc.scalar.copy(z[:], planes[h][:].rearrange("p t j -> p j t"))
-            z_c, z_s = quantize("z%d" % h, z[:].rearrange("p j t -> p (j t)"), HALF)
-            for b in range(2):
-                acc = ps.tile([P, 2, HALF], F32, name="o_ps%d_%d" % (h, b), tag="bank%d" % (2 * h + b))
-                for u in range(2):
-                    product(acc[:, u, :], dq_w, d_sc, 2 * b + u, z_c, z_s)
-                res = tile("res%d_%d" % (h, b), [P, 2, HALF], F32)
-                if h == 1 and b == 1:
-                    nc.vector.tensor_scalar(res[:], acc[:], 0.0625, None, ALU.mult)
-                    nc.sync.dma_start(out_v[:, 2 * b : 2 * b + 2, cols], res[:])
-                elif h == 1:
-                    nc.scalar.activation(res[:], acc[:], ACT.Copy, scale=0.0625)
-                    nc.scalar.dma_start(out_v[:, 2 * b : 2 * b + 2, cols], res[:])
-                else:
-                    nc.scalar.activation(res[:], acc[:], ACT.Copy, scale=0.0625)
-                    nc.sync.dma_start(out_v[:, 2 * b : 2 * b + 2, cols], res[:])
+
+        def scale_on_scalar(dst, src):
+            nc.scalar.activation(dst, src, ACT.Copy, scale=OUT_SCALE)
+
+        def scale_on_vector(dst, src):
+            nc.vector.tensor_scalar(dst, src, OUT_SCALE, None, ALU.mult)
+
+        def last_product(z_mx, j0, j1, m0, m1, bank, scale):
+            name = "out_%d_%d" % (j0, m0)
+            acc = ps.tile([P, m1 - m0, j1 - j0], F32, name=name + "_ps", tag="bank%d" % bank)
+            for m in range(m0, m1):
+                product(acc[:, m - m0, :], dq_words, d_plane, m, z_mx[0], z_mx[1])
+            res = tile(name, [P, m1 - m0, j1 - j0], F32)
+            scale(res[:], acc[:])
+            nc.sync.dma_start(out_v[:, m0:m1, j0:j1], res[:])
+
+        quarter = HALF // 2
+        dx0 = tile("dx0", [P, PACK, HALF], F32)
+        tanh_dx0 = tile("tanh_dx0", [P, PACK, HALF], F32)
+        second_lookup(0, dx0, tanh_dx0)
+        z0 = make_z(0, tanh_dx0)
+        z0_mx = quantize_z("z0_grouped", z0, 0, HALF, nc.scalar.copy)
+        dx1 = tile("dx1", [P, PACK, HALF], F32)
+        tanh_dx1 = tile("tanh_dx1", [P, PACK, HALF], F32)
+        second_lookup(1, dx1, tanh_dx1)
+        last_product(z0_mx, 0, HALF, 0, 2, 0, scale_on_scalar)
+        last_product(z0_mx, 0, HALF, 2, 4, 1, scale_on_scalar)
+        z1 = make_z(1, tanh_dx1)
+        z1a_mx = quantize_z("z1a_grouped", z1, 0, quarter, nc.vector.tensor_copy)
+        last_product(z1a_mx, HALF, HALF + quarter, 0, 4, 2, scale_on_scalar)
+        z1b_mx = quantize_z("z1b_grouped", z1, quarter, HALF, nc.vector.tensor_copy)
+        last_product(z1b_mx, HALF + quarter, S, 0, 2, 3, scale_on_scalar)
+        last_product(z1b_mx, HALF + quarter, S, 2, 4, 0, scale_on_vector)

from contextlib import ExitStack

import concourse.mybir as mybir

K, T, S, H, G = 512, 2048, 512, 512, 2048
FLOPS = 3 * 2 * K * H * S

F32 = mybir.dt.float32
BF16 = mybir.dt.bfloat16
I32 = mybir.dt.int32
U32 = mybir.dt.uint32
U16 = mybir.dt.uint16
U8 = mybir.dt.uint8
FP8X4 = mybir.dt.float8_e4m3fn_x4
ACT = mybir.ActivationFunctionType
ALU = mybir.AluOpType

P = 128
PACK = 4
QUADRANT = 32
GROUP = 16
HALF = S // 2
DEALT = P // 2
OUT_SCALE = 0.0625


def tile_picked_symplec_none_p_kernel(
    tc, x_words, x_scales, w1, w2, gs, d_words, d_scales, offs, two, nb, kq, out
):
    nc = tc.nc
    with ExitStack() as ctx:
        sb = ctx.enter_context(tc.tile_pool(name="sb", bufs=1))
        ps = ctx.enter_context(tc.psum_pool(name="ps", bufs=1))

        def tile(name, shape, dtype, tag=None):
            return sb.tile(shape, dtype, name=name, tag=tag or name, align_bytes=64)

        def feature_tiles(name):
            return [tile("%s%d" % (name, t), [P, S], F32) for t in range(PACK)]

        def load_list(name, src):
            dst = tile(name, [P, S // GROUP], U16)
            nc.sync.dma_start(dst[:], src)
            return dst

        def load_words(name, src):
            dst = tile(name, [P, T], I32)
            nc.sync.dma_start(dst[:], src[0].rearrange("p n r -> p (n r)").bitcast(I32))
            return dst

        def load_weight_half(name, src, h):
            dst = tile(name, [P, PACK, HALF], F32)
            nc.sync.dma_start(dst[:], src.rearrange("(p j) c -> p j c", j=PACK)[:, :, h * HALF : (h + 1) * HALF])
            return dst

        def gather_packed(name, table, dtype, idx, tag=None):
            dst = tile(name, [P, S], dtype, tag)
            nc.vector.tensor_copy(dst[:], table[:].bitcast(dtype).indirect(idx[:]))
            return dst

        def cast(copy, dealt, raw, h, m0, m1):
            copy(
                dealt[:].rearrange("p (t m j) -> p m t j", t=PACK, j=PACK)[:, h * DEALT + m0 : h * DEALT + m1],
                raw[:].rearrange("p j (m t) -> p m t j", t=PACK)[:, m0:m1],
            )

        def quantize(name, src, width):
            codes = tile(name + "_codes", [P, width], U32)
            scales = tile(name + "_scales", [P, width], U8)
            nc.vector.quantize_mx(out=codes[:].bitcast(FP8X4), scales=scales[:], in_=src)
            return codes, scales

        def product(acc, lhs_words, lhs_scales, block, rhs_words, rhs_scales):
            cols = slice(block * P, (block + 1) * P)
            nc.tensor.matmul_mx(
                out=acc,
                lhsT=lhs_words[:, cols].bitcast(FP8X4),
                lhsT_scale=lhs_scales[:, cols],
                rhs=rhs_words[:].bitcast(FP8X4),
                rhs_scale=rhs_scales[:],
                start=True,
                stop=True,
            )

        zero = tile("zero", [P, 1], F32)
        nc.vector.memset(zero[:], 0.0)
        zero_bias = tile("zero_bias", [P, 1], F32)
        nc.scalar.activation(zero_bias[:], zero[:], ACT.Tanh)

        xs_table = tile("xs_table", [P, T], U8)
        ds_table = tile("ds_table", [P, G], U8)
        nc.vector.memset(ds_table[:].bitcast(I32), 0)
        d_plane = tile("d_plane", [P, H], U8)
        nc.vector.memset(d_plane[:].bitcast(I32), 0)

        offs_t = load_list("offs_t", offs)
        xs_rows = x_scales[0].bitcast(I32)
        for quad in range(P // QUADRANT):
            nc.sync.dma_start(
                xs_table[QUADRANT * quad : QUADRANT * (quad + 1), :].bitcast(I32),
                xs_rows[4 * quad : 4 * (quad + 1), :].unsqueeze(0).broadcast_to([QUADRANT // 4, 4, T // 4]),
            )
        two_t = load_list("two_t", two)
        xw_table = load_words("xw_table", x_words)
        w1_raw = [load_weight_half("w1_raw%d" % h, w1, h) for h in range(2)]
        kq_t = load_list("kq_t", kq)
        ds_rows = d_scales[0].bitcast(I32).rearrange("(g e) c -> e g c", e=2)
        for e in range(2):
            nc.sync.dma_start(ds_table[e:P:GROUP, :].bitcast(I32), ds_rows[e])
        nb_t = load_list("nb_t", nb)
        w2_raw = [load_weight_half("w2_raw%d" % h, w2, h) for h in range(2)]
        gs_t = tile("gs_t", [P, PACK], F32)
        nc.sync.dma_start(gs_t[:], gs.rearrange("(p t) o -> p (t o)", t=PACK))
        dw_table = load_words("dw_table", d_words)

        w1_dealt = tile("w1_dealt", [P, PACK * H], BF16, "dealt")
        xq_scales = gather_packed("xq_scales", xs_table, U8, offs_t)
        x2_scales = gather_packed("x2_scales", xs_table, U8, two_t)
        xq_words = gather_packed("xq_words", xw_table, U32, offs_t)
        x2_words = gather_packed("x2_words", xw_table, U32, two_t, "picked_words")
        cast(nc.scalar.copy, w1_dealt, w1_raw[0], 0, 0, DEALT)
        cast(nc.scalar.copy, w1_dealt, w1_raw[1], 1, 0, DEALT // 2)
        cast(nc.vector.tensor_copy, w1_dealt, w1_raw[1], 1, DEALT // 2, DEALT)
        w1_codes, w1_scales = quantize("w1", w1_dealt[:], H)
        dq_scales = gather_packed("dq_scales", ds_table, U8, kq_t)
        w2_dealt = tile("w2_dealt", [P, PACK * H], BF16, "dealt")
        cast(nc.scalar.copy, w2_dealt, w2_raw[0], 0, 0, DEALT)
        cast(nc.vector.tensor_copy, w2_dealt, w2_raw[1], 1, 0, DEALT)

        y_ps = [ps.tile([P, S], F32, name="y_ps%d" % t, tag="bank%d" % t) for t in range(PACK)]
        c_ps = [ps.tile([P, S], F32, name="c_ps%d" % t) for t in range(PACK)]
        for t in range(PACK):
            product(y_ps[t][:], w1_codes, w1_scales, t, xq_words, xq_scales)

        y_window = [tile("y_window%d" % t, [P, S if t == 0 else 2 * S], F32) for t in range(PACK)]
        y_last = tile("y_last", [P, S], F32)
        y_own = [y_window[t + 1][:, S:] for t in range(PACK - 1)] + [y_last[:]]
        dy, tanh_dy, vn, bracket, gs_vn = (feature_tiles(name) for name in ("dy", "tanh_dy", "vn", "bracket", "gs_vn"))
        halves = [slice(h * HALF, (h + 1) * HALF) for h in range(2)]
        nb_half = [nb_t[:, h * HALF // GROUP : (h + 1) * HALF // GROUP] for h in range(2)]

        nc.scalar.copy(y_window[0][:], y_ps[0][:])
        for h in range(2):
            nc.scalar.copy(y_own[0][:, halves[h]], y_ps[0][:, halves[h]])
            nc.vector.tensor_tensor(
                dy[0][:, halves[h]], y_window[0][:].indirect(nb_half[h]), y_own[0][:, halves[h]], ALU.subtract
            )
        w2_codes, w2_scales = quantize("w2", w2_dealt[:], H)
        for t in range(1, PACK):
            nc.scalar.copy(y_window[t][:, :S], y_ps[t][:])
            nc.scalar.copy(y_own[t], y_ps[t][:])
            nc.vector.tensor_tensor(dy[t][:], y_window[t][:].indirect(nb_t[:]), y_own[t], ALU.subtract)
        for t in range(PACK):
            product(c_ps[t][:], w2_codes, w2_scales, t, x2_words, x2_scales)

        for t in range(PACK):
            nc.scalar.activation(tanh_dy[t][:], dy[t][:], ACT.Tanh, bias=zero_bias[:])
            nc.vector.tensor_tensor(vn[t][:], c_ps[t][:], tanh_dy[t][:], ALU.add)
        for t in range(PACK):
            nc.vector.scalar_tensor_tensor(bracket[t][:], dy[t][:], -2.0, vn[t][:], ALU.mult, ALU.add)
            nc.scalar.activation(gs_vn[t][:], vn[t][:], ACT.Copy, scale=gs_t[:, t : t + 1])

        dq_words = gather_packed("dq_words", dw_table, U32, kq_t, "picked_words")
        for r in range(4):
            src = GROUP * (r // 2) + r % 2
            nc.sync.dma_start(d_plane[r:P:QUADRANT, :].bitcast(I32), dq_scales[src:P:QUADRANT, :].bitcast(I32))

        def second_lookup(h, dx, tanh_dx):
            for t in range(PACK):
                nc.vector.tensor_tensor(dx[:, t, :], vn[t][:].indirect(nb_half[h]), bracket[t][:, halves[h]], ALU.subtract)
                nc.scalar.activation(tanh_dx[:, t, :], dx[:, t, :], ACT.Tanh, bias=zero_bias[:], scale=0.5)

        def make_z(h, tanh_dx):
            z = tile("z%d" % h, [P, PACK, HALF], BF16)
            for t in range(PACK):
                nc.vector.scalar_tensor_tensor(
                    z[:, t, :], tanh_dx[:, t, :], gs_t[:, t : t + 1], gs_vn[t][:, halves[h]], ALU.mult, ALU.add
                )
            return z

        def quantize_z(name, z, j0, j1, copy):
            grouped = tile(name, [P, j1 - j0, PACK], BF16)
            copy(grouped[:], z[:, :, j0:j1].rearrange("p t j -> p j t"))
            return quantize(name, grouped[:].rearrange("p j t -> p (j t)"), j1 - j0)

        out_v = out.rearrange("(m p) j -> p m j", p=P)

        def scale_on_scalar(dst, src):
            nc.scalar.activation(dst, src, ACT.Copy, scale=OUT_SCALE)

        def scale_on_vector(dst, src):
            nc.vector.tensor_scalar(dst, src, OUT_SCALE, None, ALU.mult)

        def last_product(z_mx, j0, j1, m0, m1, bank, scale):
            name = "out_%d_%d" % (j0, m0)
            acc = ps.tile([P, m1 - m0, j1 - j0], F32, name=name + "_ps", tag="bank%d" % bank)
            for m in range(m0, m1):
                product(acc[:, m - m0, :], dq_words, d_plane, m, z_mx[0], z_mx[1])
            res = tile(name, [P, m1 - m0, j1 - j0], F32)
            scale(res[:], acc[:])
            nc.sync.dma_start(out_v[:, m0:m1, j0:j1], res[:])

        quarter = HALF // 2
        dx0 = tile("dx0", [P, PACK, HALF], F32)
        tanh_dx0 = tile("tanh_dx0", [P, PACK, HALF], F32)
        second_lookup(0, dx0, tanh_dx0)
        z0 = make_z(0, tanh_dx0)
        z0_mx = quantize_z("z0_grouped", z0, 0, HALF, nc.scalar.copy)
        dx1 = tile("dx1", [P, PACK, HALF], F32)
        tanh_dx1 = tile("tanh_dx1", [P, PACK, HALF], F32)
        second_lookup(1, dx1, tanh_dx1)
        last_product(z0_mx, 0, HALF, 0, 2, 0, scale_on_scalar)
        last_product(z0_mx, 0, HALF, 2, 4, 1, scale_on_scalar)
        z1 = make_z(1, tanh_dx1)
        z1a_mx = quantize_z("z1a_grouped", z1, 0, quarter, nc.vector.tensor_copy)
        last_product(z1a_mx, HALF, HALF + quarter, 0, 4, 2, scale_on_scalar)
        z1b_mx = quantize_z("z1b_grouped", z1, quarter, HALF, nc.vector.tensor_copy)
        last_product(z1b_mx, HALF + quarter, S, 0, 2, 3, scale_on_scalar)
        last_product(z1b_mx, HALF + quarter, S, 2, 4, 0, scale_on_vector)
